import numpy as np
import ml_dtypes


def mxq(x, axis, fmt="e4m3"):
    dtype, down = {"e4m3": (ml_dtypes.float8_e4m3fn, 7), "e5m2": (ml_dtypes.float8_e5m2, 14)}[fmt]
    v = np.moveaxis(np.asarray(x, np.float32).astype(ml_dtypes.bfloat16).astype(np.float64), axis, -1)
    blocks = v.reshape(v.shape[:-1] + (-1, 32))
    amax = np.abs(blocks).max(-1, keepdims=True)
    byte = np.maximum(np.where(amax > 0, np.frexp(amax)[1] - 1 + 127, 0) - down, 1)
    scale = np.exp2(byte - 127.0)
    codes = (blocks / scale).astype(np.float32).astype(dtype).astype(np.float64)
    return np.moveaxis((codes * scale).reshape(v.shape), -1, axis)


WIDE = False


def mx_kscale(k):
    if not WIDE:
        return np.ones(k)
    levels = np.array([10, -10, 5, -5, 0])
    if k % 512:
        return np.exp2(np.random.permutation(np.resize(levels, k // 32))).repeat(32)
    a = np.empty((k // 512, 16))
    for p in range(k // 512):
        a[p, :8] = np.random.permutation(np.resize(levels, 8))
        for g in range(8):
            far = levels[np.abs(levels - a[p, g]) >= 10]
            a[p, g + 8] = far[np.random.randint(len(far))]
    return np.exp2(a.ravel()).repeat(32)


def f64(x):
    return np.asarray(x).astype(np.float64)


def striped(idx):
    return np.tile(idx.reshape(-1, 16).T, (8, 1)).astype(np.uint16)


def unstriped(offs):
    return offs[:16].T.reshape(-1).astype(np.int64)


E2M1 = np.array([0.0, 0.5, 1.0, 1.5, 2.0, 3.0, 4.0, 6.0, -0.0, -0.5, -1.0, -1.5, -2.0, -3.0, -4.0, -6.0])


def pack_weight(w, fmt):
    k, n = w.shape
    w = f64(np.asarray(w, np.float32).astype(ml_dtypes.bfloat16)).reshape(k // 32, 32, n)
    amax = np.abs(w).max(1)
    if fmt == "e4m3":
        byte = np.frexp(amax)[1] - 1 + 127 - 7
    else:
        mant, ex = np.frexp(amax / 6.0)
        byte = np.where(mant > 0.5, ex, ex - 1) + 127
    byte = np.clip(np.where(amax > 0, byte, 1), 1, 254)
    scaled = (w * np.exp2(127.0 - byte)[:, None, :]).reshape(k, n).astype(np.float32)
    by_word = np.ascontiguousarray(scaled.reshape(k // 512, 128, 4, n).transpose(0, 1, 3, 2))
    if fmt == "e4m3":
        words = by_word.astype(ml_dtypes.float8_e4m3fn).view(np.uint8)
    else:
        c = by_word.astype(ml_dtypes.float4_e2m1fn).view(np.uint8) & 0xF
        words = (c[..., 0::2] | (c[..., 1::2] << 4)).reshape(k // 512, 128, 2 * n)
    return np.ascontiguousarray(words), np.ascontiguousarray(byte.astype(np.uint8).reshape(k // 512, 16, n))


def unpack_weight(words, scales, fmt):
    g, _, n = scales.shape
    words = np.ascontiguousarray(words).reshape(g, 128, n, -1)
    if fmt == "e4m3":
        vals = words.view(ml_dtypes.float8_e4m3fn).astype(np.float64)
    else:
        nib = np.empty((g, 128, n, 4), np.uint8)
        nib[..., 0::2] = words & 0xF
        nib[..., 1::2] = words >> 4
        vals = E2M1[nib]
    vals = vals * np.repeat(np.exp2(scales.astype(np.float64) - 127.0), 8, axis=1)[..., None]
    return vals.transpose(0, 1, 3, 2).reshape(g * 512, n)


K, T, E, C, N = 1024, 2048, 8, 128, 384


def by_expert(wq, xq):
    return np.concatenate([wq[e].T @ xq[:, e * C:(e + 1) * C] for e in range(E)], axis=1)


def setup_inputs():
    n = np.random.standard_normal
    s = mx_kscale(K)[:, None]
    x = pack_weight(n((K, T)) * s, "e4m3")
    return {
        "x_words": x[0],
        "x_scales": x[1],
        "w": (n((E + 1, K, N)) / np.sqrt(K) / s[None]).astype(np.float32),
        "gate": np.tile(np.random.uniform(0.2, 1.0, E * C), (N, 1)).astype(np.float32),
        "offs": striped(np.random.permutation(T)[:E * C]),
    }


def reference(x_words, x_scales, w, gate, offs):
    idx = unstriped(offs)
    wq = mxq(f64(w), 1, "e4m3")
    xs = unpack_weight(x_words, x_scales, "e4m3")
    ys = wq[E].T @ xs
    xq = unpack_weight(x_words, x_scales, "e4m3")[:, idx]
    y = by_expert(wq, xq)
    out = ys
    out[:, idx] += f64(gate) * y
    return out

@@ -1,0 +1,179 @@
+from contextlib import ExitStack
+
+import concourse.mybir as mybir
+
+K, T, E, C, N = 1024, 2048, 8, 128, 384
+S = E * C
+FLOPS = 2 * K * N * (S + T)
+BYTES = K * T + K * T // 32 + 4 * (E + 1) * K * N + 4 * S + 2 * S + 4 * N * T
+
+F32 = mybir.dt.float32
+BF16 = mybir.dt.bfloat16
+I32 = mybir.dt.int32
+U32 = mybir.dt.uint32
+U16 = mybir.dt.uint16
+U8 = mybir.dt.uint8
+FP8X4 = mybir.dt.float8_e4m3fn_x4
+MULT = mybir.AluOpType.mult
+ADD = mybir.AluOpType.add
+
+P = 128
+PACK = 4
+PASSES = K // (P * PACK)
+BLOCKS = N // P
+BANK = 512
+PAIR = 2 * C
+PAIRS = E // 2
+HALF = PACK * N
+
+
+def tile_moe_shr_lin_none_kernel(tc, x_words, x_scales, w, gate, offs, out):
+    nc = tc.nc
+    with ExitStack() as ctx:
+        keep = ctx.enter_context(tc.tile_pool(name="keep", bufs=1))
+        raw_pool = ctx.enter_context(tc.tile_pool(name="raw", bufs=12))
+        ring = ctx.enter_context(tc.tile_pool(name="ring", bufs=2))
+        y_psum = ctx.enter_context(tc.psum_pool(name="y_psum", bufs=1))
+        s_psum = ctx.enter_context(tc.psum_pool(name="s_psum", bufs=5))
+
+        offsets = keep.tile([P, S // 16], U16, name="offsets")
+        words = [keep.tile([P, T], I32, name="words%d" % o, align_bytes=64) for o in range(PASSES)]
+        scales = keep.tile([P, T], U8, name="scales", align_bytes=64)
+        slot_words = [keep.tile([P, S], U32, name="slot_words%d" % o, align_bytes=64) for o in range(PASSES)]
+        slot_scales = keep.tile([P, S], U8, name="slot_scales", align_bytes=64)
+        gates = [keep.tile([P, PAIR], F32, name="gates%d" % k) for k in range(PAIRS)]
+        routed = [keep.tile([P, T], F32, name="routed%d" % b) for b in range(BLOCKS)]
+        result = [keep.tile([P, T], F32, name="result%d" % b) for b in range(BLOCKS)]
+
+        raw = {}
+
+        def load_weights(e, o):
+            if (e, o) == (E, PASSES - 1):
+                raw[e, o] = keep.tile([P, HALF], F32, name="last_raw", tag="last")
+            else:
+                raw[e, o] = raw_pool.tile([P, HALF], F32, name="raw")
+            rows = w[e, o * P * PACK : (o + 1) * P * PACK, :]
+            nc.sync.dma_start(out=raw[e, o][:], in_=rows.rearrange("(p j) n -> p (j n)", j=PACK))
+
+        def load_words(o):
+            nc.sync.dma_start(out=words[o][:], in_=x_words[o].rearrange("p t r -> p (t r)").bitcast(I32))
+
+        def load_scales():
+            for q in range(4):
+                nc.sync.dma_start(
+                    out=scales[:].bitcast(I32)[32 * q : 32 * q + 4 * PASSES, :],
+                    in_=x_scales[:, 4 * q : 4 * q + 4, :].bitcast(I32),
+                )
+
+        def load_gates(k):
+            nc.sync.dma_start(out=gates[k][:], in_=gate[0:P, k * PAIR : (k + 1) * PAIR])
+
+        def cast(engine_copy, dst, e, o, lo, hi):
+            src = raw[e, o][:].rearrange("p (t n) -> p t n", t=PACK)[:, :, lo:hi]
+            engine_copy(
+                out=dst[:, PACK * lo : PACK * hi].rearrange("p (c i t) -> p c t i", i=4, t=PACK),
+                in_=src.rearrange("p t (c i) -> p c t i", i=4),
+            )
+
+        def quantize(codes, plane, at, grouped, widths):
+            lo = 0
+            for width in widths:
+                nc.vector.quantize_mx(
+                    out=codes[:, at + lo : at + lo + width].bitcast(FP8X4),
+                    scales=plane[:, at + lo : at + lo + width],
+                    in_=grouped[:, PACK * lo : PACK * (lo + width)],
+                )
+                lo = lo + width
+
+        def multiply(acc, codes, plane, at, rhs_words, rhs_scales, cols, o):
+            nc.tensor.matmul_mx(
+                out=acc,
+                lhsT=codes[:, at : at + P].bitcast(FP8X4),
+                lhsT_scale=plane[:, at : at + P],
+                rhs=rhs_words[o][:, cols].bitcast(FP8X4),
+                rhs_scale=rhs_scales[4 * o : P, cols],
+                start=(o == 0),
+                stop=(o == PASSES - 1),
+            )
+
+        nc.vector.memset(scales[:].bitcast(I32), 0)
+        nc.sync.dma_start(offsets[:], offs)
+        load_words(0)
+        load_weights(0, 0)
+        load_scales()
+        load_words(1)
+        load_weights(0, 1)
+        load_weights(1, 0)
+        load_weights(1, 1)
+        load_gates(0)
+        for k in range(1, PAIRS):
+            for e in (2 * k, 2 * k + 1):
+                for o in range(PASSES):
+                    load_weights(e, o)
+            load_gates(k)
+        for o in range(PASSES):
+            load_weights(E, o)
+
+        for b in range(BLOCKS):
+            nc.gpsimd.memset(routed[b][:], 0.0)
+        for o in range(PASSES):
+            nc.vector.tensor_copy(slot_words[o][:], words[o][:].bitcast(U32).indirect(offsets[:]))
+        nc.vector.tensor_copy(slot_scales[:], scales[:].indirect(offsets[:]))
+
+        def first_half(e, engine_copy):
+            codes = ring.tile([P, 4 * N], U32, name="codes", align_bytes=64)
+            plane = ring.tile([P, 4 * N], U8, name="plane", align_bytes=64)
+            edge = keep.tile([P, HALF], BF16, name="edge", tag="edge", align_bytes=64)
+            cast(engine_copy, edge, e, 0, 0, N)
+            quantize(codes, plane, 0, edge, (256, 128))
+            return codes, plane
+
+        codes, plane = first_half(0, nc.scalar.copy)
+        for k in range(PAIRS):
+            e = 2 * k
+            middle = ring.tile([P, 2 * HALF], BF16, name="middle", align_bytes=64)
+            cast(nc.scalar.copy, middle[:, 0:HALF], e, 1, 0, N)
+            cast(nc.scalar.copy, middle[:, HALF : 2 * HALF], e + 1, 0, 0, N)
+            quantize(codes, plane, N, middle, (512, 256))
+            edge = keep.tile([P, HALF], BF16, name="edge", tag="edge", align_bytes=64)
+            if k == 0:
+                cast(nc.scalar.copy, edge, e + 1, 1, 0, 128)
+                cast(nc.vector.tensor_copy, edge, e + 1, 1, 128, N)
+            else:
+                cast(nc.scalar.copy, edge, e + 1, 1, 0, N)
+            quantize(codes, plane, 3 * N, edge, (256, 128))
+
+            acc = [y_psum.tile([P, PAIR], F32, name="acc%d" % b) for b in range(BLOCKS)]
+            for h in range(2):
+                for o in range(PASSES):
+                    for b in range(BLOCKS):
+                        slots = slice((e + h) * C, (e + h + 1) * C)
+                        at = (2 * h + o) * N + b * P
+                        multiply(acc[b][:, h * C : (h + 1) * C], codes, plane, at, slot_words, slot_scales, slots, o)
+
+            codes, plane = first_half(e + 2, nc.vector.tensor_copy)
+            ys = [ring.tile([P, PAIR], F32, name="y0")]
+            nc.scalar.copy(out=ys[0][:], in_=acc[0][:])
+            if k == PAIRS - 1:
+                middle = ring.tile([P, 2 * HALF], BF16, name="middle", align_bytes=64)
+                cast(nc.scalar.copy, middle[:, 0:HALF], E, 1, 0, N)
+                quantize(codes, plane, N, middle, (256, 128))
+                rest = keep.tile([P, 2 * PAIR], F32, name="last_y", tag="last")
+            else:
+                rest = ring.tile([P, 2 * PAIR], F32, name="y12")
+            for b in range(1, BLOCKS):
+                ys.append(rest[:, (b - 1) * PAIR : b * PAIR])
+                nc.scalar.copy(out=ys[b], in_=acc[b][:])
+            for b in range(BLOCKS):
+                nc.vector.tensor_tensor(
+                    routed[b][:].indirect(offsets[:, k * PAIR // 16 : (k + 1) * PAIR // 16]), ys[b][:], gates[k][:], MULT
+                )
+
+        for b in range(BLOCKS):
+            for c in range(T // BANK):
+                tokens = slice(c * BANK, (c + 1) * BANK)
+                shared = s_psum.tile([P, BANK], F32, name="shared")
+                for o in range(PASSES):
+                    multiply(shared[:], codes, plane, o * N + b * P, words, scales, tokens, o)
+                nc.vector.tensor_tensor(result[b][:, tokens], shared[:], routed[b][:, tokens], ADD)
+                nc.sync.dma_start(out=out[b * P : (b + 1) * P, tokens], in_=result[b][:, tokens])

@@ -31,8 +31,8 @@ def tile_moe_shr_lin_none_kernel(tc, x_words, x_scales, w, gate, offs, out):
     nc = tc.nc
     with ExitStack() as ctx:
         keep = ctx.enter_context(tc.tile_pool(name="keep", bufs=1))
-        raw_pool = ctx.enter_context(tc.tile_pool(name="raw", bufs=12))
-        ring = ctx.enter_context(tc.tile_pool(name="ring", bufs=2))
+        raw_pool = ctx.enter_context(tc.tile_pool(name="raw", bufs=18))
+        ring = ctx.enter_context(tc.tile_pool(name="ring", bufs=3))
         y_psum = ctx.enter_context(tc.psum_pool(name="y_psum", bufs=1))
         s_psum = ctx.enter_context(tc.psum_pool(name="s_psum", bufs=5))
 
@@ -48,21 +48,18 @@ def tile_moe_shr_lin_none_kernel(tc, x_words, x_scales, w, gate, offs, out):
         raw = {}
 
         def load_weights(e, o):
-            if (e, o) == (E, PASSES - 1):
-                raw[e, o] = keep.tile([P, HALF], F32, name="last_raw", tag="last")
-            else:
-                raw[e, o] = raw_pool.tile([P, HALF], F32, name="raw")
+            raw[e, o] = raw_pool.tile([P, HALF], F32, name="raw")
             rows = w[e, o * P * PACK : (o + 1) * P * PACK, :]
             nc.sync.dma_start(out=raw[e, o][:], in_=rows.rearrange("(p j) n -> p (j n)", j=PACK))
 
         def load_words(o):
             nc.sync.dma_start(out=words[o][:], in_=x_words[o].rearrange("p t r -> p (t r)").bitcast(I32))
 
-        def load_scales():
-            for q in range(4):
+        def load_scales(o):
+            for r in range(4):
                 nc.sync.dma_start(
-                    out=scales[:].bitcast(I32)[32 * q : 32 * q + 4 * PASSES, :],
-                    in_=x_scales[:, 4 * q : 4 * q + 4, :].bitcast(I32),
+                    out=scales[:].bitcast(I32)[4 * o + r : P : 32, :],
+                    in_=x_scales[o, r:16:4, :].bitcast(I32),
                 )
 
         def load_gates(k):
@@ -75,15 +72,10 @@ def tile_moe_shr_lin_none_kernel(tc, x_words, x_scales, w, gate, offs, out):
                 in_=src.rearrange("p t (c i) -> p c t i", i=4),
             )
 
-        def quantize(codes, plane, at, grouped, widths):
-            lo = 0
-            for width in widths:
-                nc.vector.quantize_mx(
-                    out=codes[:, at + lo : at + lo + width].bitcast(FP8X4),
-                    scales=plane[:, at + lo : at + lo + width],
-                    in_=grouped[:, PACK * lo : PACK * (lo + width)],
-                )
-                lo = lo + width
+        def quantize(codes, plane, grouped, lo, hi):
+            nc.vector.quantize_mx(
+                out=codes[:, lo:hi].bitcast(FP8X4), scales=plane[:, lo:hi], in_=grouped[:, PACK * lo : PACK * hi]
+            )
 
         def multiply(acc, codes, plane, at, rhs_words, rhs_scales, cols, o):
             nc.tensor.matmul_mx(
@@ -99,9 +91,10 @@ def tile_moe_shr_lin_none_kernel(tc, x_words, x_scales, w, gate, offs, out):
         nc.vector.memset(scales[:].bitcast(I32), 0)
         nc.sync.dma_start(offsets[:], offs)
         load_words(0)
-        load_weights(0, 0)
-        load_scales()
+        load_scales(0)
         load_words(1)
+        load_weights(0, 0)
+        load_scales(1)
         load_weights(0, 1)
         load_weights(1, 0)
         load_weights(1, 1)
@@ -114,66 +107,78 @@ def tile_moe_shr_lin_none_kernel(tc, x_words, x_scales, w, gate, offs, out):
         for o in range(PASSES):
             load_weights(E, o)
 
-        for b in range(BLOCKS):
-            nc.gpsimd.memset(routed[b][:], 0.0)
+        nc.vector.memset(routed[0][:], 0.0)
+        for b in range(1, BLOCKS):
+            nc.scalar.copy(out=routed[b][:], in_=routed[0][:])
         for o in range(PASSES):
             nc.vector.tensor_copy(slot_words[o][:], words[o][:].bitcast(U32).indirect(offsets[:]))
         nc.vector.tensor_copy(slot_scales[:], scales[:].indirect(offsets[:]))
 
-        def first_half(e, engine_copy):
-            codes = ring.tile([P, 4 * N], U32, name="codes", align_bytes=64)
-            plane = ring.tile([P, 4 * N], U8, name="plane", align_bytes=64)
-            edge = keep.tile([P, HALF], BF16, name="edge", tag="edge", align_bytes=64)
-            cast(engine_copy, edge, e, 0, 0, N)
-            quantize(codes, plane, 0, edge, (256, 128))
-            return codes, plane
+        codes = {}
+        planes = {}
+        acc = {}
+        grouped = {}
 
-        codes, plane = first_half(0, nc.scalar.copy)
-        for k in range(PAIRS):
-            e = 2 * k
-            middle = ring.tile([P, 2 * HALF], BF16, name="middle", align_bytes=64)
-            cast(nc.scalar.copy, middle[:, 0:HALF], e, 1, 0, N)
-            cast(nc.scalar.copy, middle[:, HALF : 2 * HALF], e + 1, 0, 0, N)
-            quantize(codes, plane, N, middle, (512, 256))
-            edge = keep.tile([P, HALF], BF16, name="edge", tag="edge", align_bytes=64)
-            if k == 0:
-                cast(nc.scalar.copy, edge, e + 1, 1, 0, 128)
-                cast(nc.vector.tensor_copy, edge, e + 1, 1, 128, N)
+        def prepare(e, o):
+            if o == 0:
+                codes[e] = ring.tile([P, PASSES * N], U32, name="codes", align_bytes=64)
+                planes[e] = ring.tile([P, PASSES * N], U8, name="plane", align_bytes=64)
+                grouped[e] = ring.tile([P, PASSES * HALF], BF16, name="grouped", align_bytes=64)
+            half = grouped[e][:, o * HALF : (o + 1) * HALF]
+            if (e, o) == (1, 1):
+                cast(nc.scalar.copy, half, e, o, 0, 128)
+                cast(nc.vector.tensor_copy, half, e, o, 128, N)
             else:
-                cast(nc.scalar.copy, edge, e + 1, 1, 0, N)
-            quantize(codes, plane, 3 * N, edge, (256, 128))
-
-            acc = [y_psum.tile([P, PAIR], F32, name="acc%d" % b) for b in range(BLOCKS)]
-            for h in range(2):
-                for o in range(PASSES):
-                    for b in range(BLOCKS):
-                        slots = slice((e + h) * C, (e + h + 1) * C)
-                        at = (2 * h + o) * N + b * P
-                        multiply(acc[b][:, h * C : (h + 1) * C], codes, plane, at, slot_words, slot_scales, slots, o)
-
-            codes, plane = first_half(e + 2, nc.vector.tensor_copy)
-            ys = [ring.tile([P, PAIR], F32, name="y0")]
-            nc.scalar.copy(out=ys[0][:], in_=acc[0][:])
-            if k == PAIRS - 1:
-                middle = ring.tile([P, 2 * HALF], BF16, name="middle", align_bytes=64)
-                cast(nc.scalar.copy, middle[:, 0:HALF], E, 1, 0, N)
-                quantize(codes, plane, N, middle, (256, 128))
-                rest = keep.tile([P, 2 * PAIR], F32, name="last_y", tag="last")
+                cast(nc.scalar.copy, half, e, o, 0, N)
+            if o == 0:
+                quantize(codes[e], planes[e], grouped[e], 0, 256)
             else:
-                rest = ring.tile([P, 2 * PAIR], F32, name="y12")
-            for b in range(1, BLOCKS):
-                ys.append(rest[:, (b - 1) * PAIR : b * PAIR])
-                nc.scalar.copy(out=ys[b], in_=acc[b][:])
-            for b in range(BLOCKS):
-                nc.vector.tensor_tensor(
-                    routed[b][:].indirect(offsets[:, k * PAIR // 16 : (k + 1) * PAIR // 16]), ys[b][:], gates[k][:], MULT
-                )
+                quantize(codes[e], planes[e], grouped[e], 256, 768)
+            if e < E and o == PASSES - 1:
+                k, h = divmod(e, 2)
+                slots = slice(e * C, (e + 1) * C)
+                for b in range(BLOCKS):
+                    if h == 0:
+                        acc[k, b] = y_psum.tile([P, PAIR], F32, name="acc%d" % b)
+                    for a in range(PASSES):
+                        multiply(acc[k, b][:, h * C : (h + 1) * C], codes[e], planes[e], a * N + b * P, slot_words, slot_scales, slots, a)
 
-        for b in range(BLOCKS):
+        def scatter(k, b, y):
+            nc.scalar.copy(out=y, in_=acc[k, b][:])
+            nc.vector.tensor_tensor(
+                routed[b][:].indirect(offsets[:, k * PAIR // 16 : (k + 1) * PAIR // 16]), y, gates[k][:], MULT
+            )
+
+        def combine(b, stores):
+            done = 0
             for c in range(T // BANK):
                 tokens = slice(c * BANK, (c + 1) * BANK)
                 shared = s_psum.tile([P, BANK], F32, name="shared")
                 for o in range(PASSES):
-                    multiply(shared[:], codes, plane, o * N + b * P, words, scales, tokens, o)
-                nc.vector.tensor_tensor(result[b][:, tokens], shared[:], routed[b][:, tokens], ADD)
-                nc.sync.dma_start(out=out[b * P : (b + 1) * P, tokens], in_=result[b][:, tokens])
+                    multiply(shared[:], codes[E], planes[E], o * N + b * P, words, scales, tokens, o)
+                cuts = [c * BANK] + [x for x in stores if c * BANK < x < (c + 1) * BANK] + [(c + 1) * BANK]
+                for lo, hi in zip(cuts, cuts[1:]):
+                    nc.vector.tensor_tensor(
+                        result[b][:, lo:hi], shared[:, lo - c * BANK : hi - c * BANK], routed[b][:, lo:hi], ADD
+                    )
+                    if hi in stores:
+                        nc.sync.dma_start(out=out[b * P : (b + 1) * P, done:hi], in_=result[b][:, done:hi])
+                        done = hi
+
+        for e in range(2):
+            for o in range(PASSES):
+                prepare(e, o)
+        for k in range(PAIRS):
+            e = 2 * k + 2
+            prepare(e, 0)
+            scatter(k, 0, raw[e, 0][:, 0:PAIR])
+            prepare(e, 1)
+            scatter(k, 1, raw[e, 1][:, 0:PAIR])
+            if e < E:
+                prepare(e + 1, 0)
+                prepare(e + 1, 1)
+                scatter(k, 2, raw[e + 1, 1][:, 0:PAIR])
+        combine(0, (1024, 2048))
+        scatter(PAIRS - 1, 2, routed[0][:, 0:PAIR])
+        combine(1, (1024, 2048))
+        combine(2, (1024, 1536, 1792, 2048))

@@ -25,6 +25,7 @@ BANK = 512
 PAIR = 2 * C
 PAIRS = E // 2
 HALF = PACK * N
+VECTOR_SHARE = {(1, 1): 256, (3, 1): 256, (4, 0): 96, (6, 0): 96}
 
 
 def tile_moe_shr_lin_none_kernel(tc, x_words, x_scales, w, gate, offs, out):
@@ -125,11 +126,11 @@ def tile_moe_shr_lin_none_kernel(tc, x_words, x_scales, w, gate, offs, out):
                 planes[e] = ring.tile([P, PASSES * N], U8, name="plane", align_bytes=64)
                 grouped[e] = ring.tile([P, PASSES * HALF], BF16, name="grouped", align_bytes=64)
             half = grouped[e][:, o * HALF : (o + 1) * HALF]
-            if (e, o) == (1, 1):
-                cast(nc.scalar.copy, half, e, o, 0, 128)
-                cast(nc.vector.tensor_copy, half, e, o, 128, N)
-            else:
-                cast(nc.scalar.copy, half, e, o, 0, N)
+            split = N - VECTOR_SHARE.get((e, o), 0)
+            if split > 0:
+                cast(nc.scalar.copy, half, e, o, 0, split)
+            if split < N:
+                cast(nc.vector.tensor_copy, half, e, o, split, N)
             if o == 0:
                 quantize(codes[e], planes[e], grouped[e], 0, 256)
             else:
@@ -144,31 +145,41 @@ def tile_moe_shr_lin_none_kernel(tc, x_words, x_scales, w, gate, offs, out):
                         multiply(acc[k, b][:, h * C : (h + 1) * C], codes[e], planes[e], a * N + b * P, slot_words, slot_scales, slots, a)
 
         def scatter(k, b, y):
-            nc.scalar.copy(out=y, in_=acc[k, b][:])
+            empty = nc.vector.tensor_copy if (k, b) == (0, 0) else nc.scalar.copy
+            empty(out=y, in_=acc[k, b][:])
             nc.vector.tensor_tensor(
                 routed[b][:].indirect(offsets[:, k * PAIR // 16 : (k + 1) * PAIR // 16]), y, gates[k][:], MULT
             )
 
-        def combine(b, stores):
-            done = 0
-            for c in range(T // BANK):
-                tokens = slice(c * BANK, (c + 1) * BANK)
-                shared = s_psum.tile([P, BANK], F32, name="shared")
-                for o in range(PASSES):
-                    multiply(shared[:], codes[E], planes[E], o * N + b * P, words, scales, tokens, o)
-                cuts = [c * BANK] + [x for x in stores if c * BANK < x < (c + 1) * BANK] + [(c + 1) * BANK]
-                for lo, hi in zip(cuts, cuts[1:]):
+        def combine(b, c, stores, side):
+            tokens = slice(c * BANK, (c + 1) * BANK)
+            shared = s_psum.tile([P, BANK], F32, name="shared")
+            for o in range(PASSES):
+                multiply(shared[:], codes[E], planes[E], o * N + b * P, words, scales, tokens, o)
+            if side:
+                nc.scalar.copy(out=result[b][:, tokens], in_=shared[:])
+                nc.gpsimd.tensor_tensor(result[b][:, tokens], result[b][:, tokens], routed[b][:, tokens], ADD)
+            cuts = [c * BANK] + [hi for lo, hi in stores if hi < (c + 1) * BANK] + [(c + 1) * BANK]
+            for lo, hi in zip(cuts, cuts[1:]):
+                if not side:
                     nc.vector.tensor_tensor(
                         result[b][:, lo:hi], shared[:, lo - c * BANK : hi - c * BANK], routed[b][:, lo:hi], ADD
                     )
-                    if hi in stores:
-                        nc.sync.dma_start(out=out[b * P : (b + 1) * P, done:hi], in_=result[b][:, done:hi])
-                        done = hi
+                for first, last in stores:
+                    if last == hi:
+                        nc.sync.dma_start(out=out[b * P : (b + 1) * P, first:last], in_=result[b][:, first:last])
 
         for e in range(2):
             for o in range(PASSES):
                 prepare(e, o)
-        for k in range(PAIRS):
+        scatter(0, 0, raw[1, 1][:, 0:PAIR])
+        prepare(2, 0)
+        scatter(0, 1, raw[2, 0][:, 0:PAIR])
+        prepare(2, 1)
+        prepare(3, 0)
+        prepare(3, 1)
+        scatter(0, 2, raw[3, 1][:, 0:PAIR])
+        for k in range(1, PAIRS):
             e = 2 * k + 2
             prepare(e, 0)
             scatter(k, 0, raw[e, 0][:, 0:PAIR])
@@ -178,7 +189,16 @@ def tile_moe_shr_lin_none_kernel(tc, x_words, x_scales, w, gate, offs, out):
                 prepare(e + 1, 0)
                 prepare(e + 1, 1)
                 scatter(k, 2, raw[e + 1, 1][:, 0:PAIR])
-        combine(0, (1024, 2048))
+        combine(0, 0, [], False)
+        combine(1, 0, [], True)
+        combine(0, 1, [(0, 1024)], False)
+        combine(1, 1, [(0, 1024)], True)
+        combine(0, 2, [], False)
+        combine(0, 3, [(1024, 2048)], False)
         scatter(PAIRS - 1, 2, routed[0][:, 0:PAIR])
-        combine(1, (1024, 2048))
-        combine(2, (1024, 1536, 1792, 2048))
+        combine(1, 2, [(1024, 1536)], False)
+        combine(1, 3, [(1536, 2048)], False)
+        combine(2, 0, [(0, 512)], False)
+        combine(2, 1, [(512, 1024)], False)
+        combine(2, 2, [(1024, 1536)], False)
+        combine(2, 3, [(1536, 1792), (1792, 2048)], False)

@@ -25,15 +25,17 @@ BANK = 512
 PAIR = 2 * C
 PAIRS = E // 2
 HALF = PACK * N
-VECTOR_SHARE = {(1, 1): 256, (3, 1): 256, (4, 0): 96, (6, 0): 96}
+NARROW = {0: (0, 256, None), 1: (256, 768, 0), 2: (768, 1024, None), 3: (1024, 1536, 1)}
+WIDE = {2: (0, 1024, 0), 3: (1024, 1536, 1)}
+VECTOR_SHARE = {(1, 1): 256, (3, 1): 256, (4, 0): 128, (6, 0): 128}
 
 
 def tile_moe_shr_lin_none_kernel(tc, x_words, x_scales, w, gate, offs, out):
     nc = tc.nc
     with ExitStack() as ctx:
         keep = ctx.enter_context(tc.tile_pool(name="keep", bufs=1))
-        raw_pool = ctx.enter_context(tc.tile_pool(name="raw", bufs=18))
-        ring = ctx.enter_context(tc.tile_pool(name="ring", bufs=3))
+        raw_pool = ctx.enter_context(tc.tile_pool(name="raw", bufs=16))
+        ring = ctx.enter_context(tc.tile_pool(name="ring", bufs=2))
         y_psum = ctx.enter_context(tc.psum_pool(name="y_psum", bufs=1))
         s_psum = ctx.enter_context(tc.psum_pool(name="s_psum", bufs=5))
 
@@ -69,8 +71,8 @@ def tile_moe_shr_lin_none_kernel(tc, x_words, x_scales, w, gate, offs, out):
         def cast(engine_copy, dst, e, o, lo, hi):
             src = raw[e, o][:].rearrange("p (t n) -> p t n", t=PACK)[:, :, lo:hi]
             engine_copy(
-                out=dst[:, PACK * lo : PACK * hi].rearrange("p (c i t) -> p c t i", i=4, t=PACK),
-                in_=src.rearrange("p t (c i) -> p c t i", i=4),
+                out=dst[:, PACK * lo : PACK * hi].rearrange("p (c i t) -> p c t i", i=2, t=PACK),
+                in_=src.rearrange("p t (c i) -> p c t i", i=2),
             )
 
         def quantize(codes, plane, grouped, lo, hi):
@@ -121,28 +123,30 @@ def tile_moe_shr_lin_none_kernel(tc, x_words, x_scales, w, gate, offs, out):
         grouped = {}
 
         def prepare(e, o):
-            if o == 0:
-                codes[e] = ring.tile([P, PASSES * N], U32, name="codes", align_bytes=64)
-                planes[e] = ring.tile([P, PASSES * N], U8, name="plane", align_bytes=64)
-                grouped[e] = ring.tile([P, PASSES * HALF], BF16, name="grouped", align_bytes=64)
-            half = grouped[e][:, o * HALF : (o + 1) * HALF]
+            k, h = divmod(e, 2)
+            step = PASSES * h + o
+            if step == 0:
+                codes[k] = ring.tile([P, 2 * PASSES * N], U32, name="codes", align_bytes=64)
+                planes[k] = ring.tile([P, 2 * PASSES * N], U8, name="plane", align_bytes=64)
+                grouped[k] = ring.tile([P, 2 * PASSES * HALF], BF16, name="grouped", align_bytes=64)
+            half = grouped[k][:, step * HALF : (step + 1) * HALF]
             split = N - VECTOR_SHARE.get((e, o), 0)
             if split > 0:
                 cast(nc.scalar.copy, half, e, o, 0, split)
             if split < N:
                 cast(nc.vector.tensor_copy, half, e, o, split, N)
-            if o == 0:
-                quantize(codes[e], planes[e], grouped[e], 0, 256)
-            else:
-                quantize(codes[e], planes[e], grouped[e], 256, 768)
-            if e < E and o == PASSES - 1:
-                k, h = divmod(e, 2)
-                slots = slice(e * C, (e + 1) * C)
-                for b in range(BLOCKS):
-                    if h == 0:
-                        acc[k, b] = y_psum.tile([P, PAIR], F32, name="acc%d" % b)
-                    for a in range(PASSES):
-                        multiply(acc[k, b][:, h * C : (h + 1) * C], codes[e], planes[e], a * N + b * P, slot_words, slot_scales, slots, a)
+            calls = WIDE if k in (2, 3) else NARROW
+            if step in calls:
+                lo, hi, ready = calls[step]
+                quantize(codes[k], planes[k], grouped[k], lo, hi)
+                if e < E and ready is not None:
+                    slots = slice((2 * k + ready) * C, (2 * k + ready + 1) * C)
+                    for b in range(BLOCKS):
+                        if ready == 0:
+                            acc[k, b] = y_psum.tile([P, PAIR], F32, name="acc%d" % b)
+                        for a in range(PASSES):
+                            at = (PASSES * ready + a) * N + b * P
+                            multiply(acc[k, b][:, ready * C : (ready + 1) * C], codes[k], planes[k], at, slot_words, slot_scales, slots, a)
 
         def scatter(k, b, y):
             empty = nc.vector.tensor_copy if (k, b) == (0, 0) else nc.scalar.copy
@@ -155,7 +159,7 @@ def tile_moe_shr_lin_none_kernel(tc, x_words, x_scales, w, gate, offs, out):
             tokens = slice(c * BANK, (c + 1) * BANK)
             shared = s_psum.tile([P, BANK], F32, name="shared")
             for o in range(PASSES):
-                multiply(shared[:], codes[E], planes[E], o * N + b * P, words, scales, tokens, o)
+                multiply(shared[:], codes[PAIRS], planes[PAIRS], o * N + b * P, words, scales, tokens, o)
             if side:
                 nc.scalar.copy(out=result[b][:, tokens], in_=shared[:])
                 nc.gpsimd.tensor_tensor(result[b][:, tokens], result[b][:, tokens], routed[b][:, tokens], ADD)
@@ -195,9 +199,9 @@ def tile_moe_shr_lin_none_kernel(tc, x_words, x_scales, w, gate, offs, out):
         combine(1, 1, [(0, 1024)], True)
         combine(0, 2, [], False)
         combine(0, 3, [(1024, 2048)], False)
-        scatter(PAIRS - 1, 2, routed[0][:, 0:PAIR])
-        combine(1, 2, [(1024, 1536)], False)
-        combine(1, 3, [(1536, 2048)], False)
+        combine(1, 2, [], False)
+        combine(1, 3, [(1024, 2048)], False)
+        scatter(PAIRS - 1, 2, routed[0][:, 1536 : 1536 + PAIR])
         combine(2, 0, [(0, 512)], False)
         combine(2, 1, [(512, 1024)], False)
         combine(2, 2, [(1024, 1536)], False)

@@ -25,30 +25,40 @@ BANK = 512
 PAIR = 2 * C
 PAIRS = E // 2
 HALF = PACK * N
-NARROW = {0: (0, 256, None), 1: (256, 768, 0), 2: (768, 1024, None), 3: (1024, 1536, 1)}
-WIDE = {2: (0, 1024, 0), 3: (1024, 1536, 1)}
-VECTOR_SHARE = {(1, 1): 256, (3, 1): 256, (4, 0): 128, (6, 0): 128}
+RAW_TILES = 16
+MATRIX_TILES = 4
+SHARED_BANKS = 5
+
+VECTOR_SHARE = {(e, e % 2): 256 if e == 1 else 128 for e in range(1, E)}
+
+QUANTISE_CUTS = (0, 256, PASSES * N)
 
 
 def tile_moe_shr_lin_none_kernel(tc, x_words, x_scales, w, gate, offs, out):
     nc = tc.nc
     with ExitStack() as ctx:
         keep = ctx.enter_context(tc.tile_pool(name="keep", bufs=1))
-        raw_pool = ctx.enter_context(tc.tile_pool(name="raw", bufs=16))
-        ring = ctx.enter_context(tc.tile_pool(name="ring", bufs=2))
+        raw_pool = ctx.enter_context(tc.tile_pool(name="raw", bufs=RAW_TILES))
+        ring = ctx.enter_context(tc.tile_pool(name="ring", bufs=MATRIX_TILES))
         y_psum = ctx.enter_context(tc.psum_pool(name="y_psum", bufs=1))
-        s_psum = ctx.enter_context(tc.psum_pool(name="s_psum", bufs=5))
+        s_psum = ctx.enter_context(tc.psum_pool(name="s_psum", bufs=SHARED_BANKS))
 
         offsets = keep.tile([P, S // 16], U16, name="offsets")
         words = [keep.tile([P, T], I32, name="words%d" % o, align_bytes=64) for o in range(PASSES)]
         scales = keep.tile([P, T], U8, name="scales", align_bytes=64)
         slot_words = [keep.tile([P, S], U32, name="slot_words%d" % o, align_bytes=64) for o in range(PASSES)]
         slot_scales = keep.tile([P, S], U8, name="slot_scales", align_bytes=64)
-        gates = [keep.tile([P, PAIR], F32, name="gates%d" % k) for k in range(PAIRS)]
+        first_gates = keep.tile([P, PAIR], F32, name="first_gates")
+        later_gates = keep.tile([P, S - PAIR], F32, name="later_gates")
+        gates = [first_gates] + [later_gates[:, k * PAIR : (k + 1) * PAIR] for k in range(PAIRS - 1)]
         routed = [keep.tile([P, T], F32, name="routed%d" % b) for b in range(BLOCKS)]
         result = [keep.tile([P, T], F32, name="result%d" % b) for b in range(BLOCKS)]
 
         raw = {}
+        grouped = {}
+        codes = {}
+        planes = {}
+        acc = {}
 
         def load_weights(e, o):
             raw[e, o] = raw_pool.tile([P, HALF], F32, name="raw")
@@ -65,9 +75,6 @@ def tile_moe_shr_lin_none_kernel(tc, x_words, x_scales, w, gate, offs, out):
                     in_=x_scales[o, r:16:4, :].bitcast(I32),
                 )
 
-        def load_gates(k):
-            nc.sync.dma_start(out=gates[k][:], in_=gate[0:P, k * PAIR : (k + 1) * PAIR])
-
         def cast(engine_copy, dst, e, o, lo, hi):
             src = raw[e, o][:].rearrange("p (t n) -> p t n", t=PACK)[:, :, lo:hi]
             engine_copy(
@@ -75,21 +82,76 @@ def tile_moe_shr_lin_none_kernel(tc, x_words, x_scales, w, gate, offs, out):
                 in_=src.rearrange("p t (c i) -> p c t i", i=2),
             )
 
-        def quantize(codes, plane, grouped, lo, hi):
-            nc.vector.quantize_mx(
-                out=codes[:, lo:hi].bitcast(FP8X4), scales=plane[:, lo:hi], in_=grouped[:, PACK * lo : PACK * hi]
-            )
-
-        def multiply(acc, codes, plane, at, rhs_words, rhs_scales, cols, o):
+        def multiply(sums, e, at, rhs_words, rhs_scales, cols, o):
             nc.tensor.matmul_mx(
-                out=acc,
-                lhsT=codes[:, at : at + P].bitcast(FP8X4),
-                lhsT_scale=plane[:, at : at + P],
+                out=sums,
+                lhsT=codes[e][:, at : at + P].bitcast(FP8X4),
+                lhsT_scale=planes[e][:, at : at + P],
                 rhs=rhs_words[o][:, cols].bitcast(FP8X4),
                 rhs_scale=rhs_scales[4 * o : P, cols],
                 start=(o == 0),
                 stop=(o == PASSES - 1),
             )
+
+        def prepare(e, o):
+            if o == 0:
+                codes[e] = ring.tile([P, PASSES * N], U32, name="codes", align_bytes=64)
+                planes[e] = ring.tile([P, PASSES * N], U8, name="plane", align_bytes=64)
+                grouped[e] = ring.tile([P, PASSES * HALF], BF16, name="grouped", align_bytes=64)
+            half = grouped[e][:, o * HALF : (o + 1) * HALF]
+            split = N - VECTOR_SHARE.get((e, o), 0)
+            cast(nc.scalar.copy, half, e, o, 0, split)
+            if split < N:
+                cast(nc.vector.tensor_copy, half, e, o, split, N)
+            lo, hi = QUANTISE_CUTS[o], QUANTISE_CUTS[o + 1]
+            nc.vector.quantize_mx(
+                out=codes[e][:, lo:hi].bitcast(FP8X4),
+                scales=planes[e][:, lo:hi],
+                in_=grouped[e][:, PACK * lo : PACK * hi],
+            )
+            if e < E and o == PASSES - 1:
+                k, h = divmod(e, 2)
+                slots = slice(e * C, (e + 1) * C)
+                for b in range(BLOCKS):
+                    if h == 0:
+                        acc[k, b] = y_psum.tile([P, PAIR], F32, name="acc%d" % b)
+                    for a in range(PASSES):
+                        multiply(acc[k, b][:, h * C : (h + 1) * C], e, a * N + b * P, slot_words, slot_scales, slots, a)
+
+        def scatter(k, b, staged, engine_copy):
+            engine_copy(out=staged, in_=acc[k, b][:])
+            nc.vector.tensor_tensor(
+                routed[b][:].indirect(offsets[:, k * PAIR // 16 : (k + 1) * PAIR // 16]), staged, gates[k][:], MULT
+            )
+
+        def shared_sums(b, c):
+            shared = s_psum.tile([P, BANK], F32, name="shared")
+            for o in range(PASSES):
+                multiply(shared[:], E, o * N + b * P, words, scales, slice(c * BANK, (c + 1) * BANK), o)
+            return shared
+
+        def add_on_vector(b, c, pieces):
+            shared = shared_sums(b, c)
+            width = BANK // pieces
+            for i in range(pieces):
+                lo = c * BANK + i * width
+                nc.vector.tensor_tensor(
+                    result[b][:, lo : lo + width],
+                    shared[:, i * width : (i + 1) * width],
+                    routed[b][:, lo : lo + width],
+                    ADD,
+                )
+                if pieces > 1:
+                    store(b, lo, lo + width)
+
+        def add_on_gpsimd(b, c):
+            shared = shared_sums(b, c)
+            tokens = slice(c * BANK, (c + 1) * BANK)
+            nc.scalar.copy(out=result[b][:, tokens], in_=shared[:])
+            nc.gpsimd.tensor_tensor(result[b][:, tokens], result[b][:, tokens], routed[b][:, tokens], ADD)
+
+        def store(b, lo, hi):
+            nc.sync.dma_start(out=out[b * P : (b + 1) * P, lo:hi], in_=result[b][:, lo:hi])
 
         nc.vector.memset(scales[:].bitcast(I32), 0)
         nc.sync.dma_start(offsets[:], offs)
@@ -101,108 +163,49 @@ def tile_moe_shr_lin_none_kernel(tc, x_words, x_scales, w, gate, offs, out):
         load_weights(0, 1)
         load_weights(1, 0)
         load_weights(1, 1)
-        load_gates(0)
-        for k in range(1, PAIRS):
-            for e in (2 * k, 2 * k + 1):
-                for o in range(PASSES):
-                    load_weights(e, o)
-            load_gates(k)
-        for o in range(PASSES):
-            load_weights(E, o)
+        nc.sync.dma_start(out=first_gates[:], in_=gate[0:P, 0:PAIR])
+        for e in range(2, E + 1):
+            for o in range(PASSES):
+                load_weights(e, o)
+            if e == 3:
+                nc.sync.dma_start(out=later_gates[:], in_=gate[0:P, PAIR:S])
 
         nc.vector.memset(routed[0][:], 0.0)
         for b in range(1, BLOCKS):
             nc.scalar.copy(out=routed[b][:], in_=routed[0][:])
+
         for o in range(PASSES):
             nc.vector.tensor_copy(slot_words[o][:], words[o][:].bitcast(U32).indirect(offsets[:]))
         nc.vector.tensor_copy(slot_scales[:], scales[:].indirect(offsets[:]))
 
-        codes = {}
-        planes = {}
-        acc = {}
-        grouped = {}
-
-        def prepare(e, o):
-            k, h = divmod(e, 2)
-            step = PASSES * h + o
-            if step == 0:
-                codes[k] = ring.tile([P, 2 * PASSES * N], U32, name="codes", align_bytes=64)
-                planes[k] = ring.tile([P, 2 * PASSES * N], U8, name="plane", align_bytes=64)
-                grouped[k] = ring.tile([P, 2 * PASSES * HALF], BF16, name="grouped", align_bytes=64)
-            half = grouped[k][:, step * HALF : (step + 1) * HALF]
-            split = N - VECTOR_SHARE.get((e, o), 0)
-            if split > 0:
-                cast(nc.scalar.copy, half, e, o, 0, split)
-            if split < N:
-                cast(nc.vector.tensor_copy, half, e, o, split, N)
-            calls = WIDE if k in (2, 3) else NARROW
-            if step in calls:
-                lo, hi, ready = calls[step]
-                quantize(codes[k], planes[k], grouped[k], lo, hi)
-                if e < E and ready is not None:
-                    slots = slice((2 * k + ready) * C, (2 * k + ready + 1) * C)
-                    for b in range(BLOCKS):
-                        if ready == 0:
-                            acc[k, b] = y_psum.tile([P, PAIR], F32, name="acc%d" % b)
-                        for a in range(PASSES):
-                            at = (PASSES * ready + a) * N + b * P
-                            multiply(acc[k, b][:, ready * C : (ready + 1) * C], codes[k], planes[k], at, slot_words, slot_scales, slots, a)
-
-        def scatter(k, b, y):
-            empty = nc.vector.tensor_copy if (k, b) == (0, 0) else nc.scalar.copy
-            empty(out=y, in_=acc[k, b][:])
-            nc.vector.tensor_tensor(
-                routed[b][:].indirect(offsets[:, k * PAIR // 16 : (k + 1) * PAIR // 16]), y, gates[k][:], MULT
-            )
-
-        def combine(b, c, stores, side):
-            tokens = slice(c * BANK, (c + 1) * BANK)
-            shared = s_psum.tile([P, BANK], F32, name="shared")
-            for o in range(PASSES):
-                multiply(shared[:], codes[PAIRS], planes[PAIRS], o * N + b * P, words, scales, tokens, o)
-            if side:
-                nc.scalar.copy(out=result[b][:, tokens], in_=shared[:])
-                nc.gpsimd.tensor_tensor(result[b][:, tokens], result[b][:, tokens], routed[b][:, tokens], ADD)
-            cuts = [c * BANK] + [hi for lo, hi in stores if hi < (c + 1) * BANK] + [(c + 1) * BANK]
-            for lo, hi in zip(cuts, cuts[1:]):
-                if not side:
-                    nc.vector.tensor_tensor(
-                        result[b][:, lo:hi], shared[:, lo - c * BANK : hi - c * BANK], routed[b][:, lo:hi], ADD
-                    )
-                for first, last in stores:
-                    if last == hi:
-                        nc.sync.dma_start(out=out[b * P : (b + 1) * P, first:last], in_=result[b][:, first:last])
-
         for e in range(2):
             for o in range(PASSES):
                 prepare(e, o)
-        scatter(0, 0, raw[1, 1][:, 0:PAIR])
+        scatter(0, 0, raw[1, 1][:, 0:PAIR], nc.vector.tensor_copy)
         prepare(2, 0)
-        scatter(0, 1, raw[2, 0][:, 0:PAIR])
+        scatter(0, 1, raw[2, 0][:, 0:PAIR], nc.scalar.copy)
         prepare(2, 1)
-        prepare(3, 0)
-        prepare(3, 1)
-        scatter(0, 2, raw[3, 1][:, 0:PAIR])
         for k in range(1, PAIRS):
-            e = 2 * k + 2
-            prepare(e, 0)
-            scatter(k, 0, raw[e, 0][:, 0:PAIR])
-            prepare(e, 1)
-            scatter(k, 1, raw[e, 1][:, 0:PAIR])
-            if e < E:
-                prepare(e + 1, 0)
-                prepare(e + 1, 1)
-                scatter(k, 2, raw[e + 1, 1][:, 0:PAIR])
-        combine(0, 0, [], False)
-        combine(1, 0, [], True)
-        combine(0, 1, [(0, 1024)], False)
-        combine(1, 1, [(0, 1024)], True)
-        combine(0, 2, [], False)
-        combine(0, 3, [(1024, 2048)], False)
-        combine(1, 2, [], False)
-        combine(1, 3, [(1024, 2048)], False)
-        scatter(PAIRS - 1, 2, routed[0][:, 1536 : 1536 + PAIR])
-        combine(2, 0, [(0, 512)], False)
-        combine(2, 1, [(512, 1024)], False)
-        combine(2, 2, [(1024, 1536)], False)
-        combine(2, 3, [(1536, 1792), (1792, 2048)], False)
+            for o in range(PASSES):
+                prepare(2 * k + 1, o)
+            scatter(k - 1, 2, raw[2 * k + 1, 1][:, 0:PAIR], nc.scalar.copy)
+            for o in range(PASSES):
+                prepare(2 * k + 2, o)
+                scatter(k, o, raw[2 * k + 2, o][:, 0:PAIR], nc.scalar.copy)
+
+        for c in range(2):
+            add_on_vector(0, c, 1)
+            add_on_gpsimd(1, c)
+        store(0, 0, T // 2)
+        for c in range(2, 4):
+            add_on_vector(0, c, 1)
+        store(0, T // 2, T)
+        for c in range(2, 4):
+            add_on_vector(1, c, 1)
+        store(1, 0, T)
+        scatter(PAIRS - 1, 2, routed[0][:, T - BANK : T - BANK + PAIR], nc.scalar.copy)
+
+        for c in range(3):
+            add_on_vector(2, c, 1)
+            store(2, c * BANK, (c + 1) * BANK)
+        add_on_vector(2, 3, 2)

from contextlib import ExitStack

import concourse.mybir as mybir

K, T, E, C, N = 1024, 2048, 8, 128, 384
S = E * C
FLOPS = 2 * K * N * (S + T)
BYTES = K * T + K * T // 32 + 4 * (E + 1) * K * N + 4 * S + 2 * S + 4 * N * T

F32 = mybir.dt.float32
BF16 = mybir.dt.bfloat16
I32 = mybir.dt.int32
U32 = mybir.dt.uint32
U16 = mybir.dt.uint16
U8 = mybir.dt.uint8
FP8X4 = mybir.dt.float8_e4m3fn_x4
MULT = mybir.AluOpType.mult
ADD = mybir.AluOpType.add

P = 128
PACK = 4
PASSES = K // (P * PACK)
BLOCKS = N // P
BANK = 512
PAIR = 2 * C
PAIRS = E // 2
HALF = PACK * N
RAW_TILES = 16
MATRIX_TILES = 4
SHARED_BANKS = 5

VECTOR_SHARE = {(e, e % 2): 256 if e == 1 else 128 for e in range(1, E)}

QUANTISE_CUTS = (0, 256, PASSES * N)


def tile_moe_shr_lin_none_kernel(tc, x_words, x_scales, w, gate, offs, out):
    nc = tc.nc
    with ExitStack() as ctx:
        keep = ctx.enter_context(tc.tile_pool(name="keep", bufs=1))
        raw_pool = ctx.enter_context(tc.tile_pool(name="raw", bufs=RAW_TILES))
        ring = ctx.enter_context(tc.tile_pool(name="ring", bufs=MATRIX_TILES))
        y_psum = ctx.enter_context(tc.psum_pool(name="y_psum", bufs=1))
        s_psum = ctx.enter_context(tc.psum_pool(name="s_psum", bufs=SHARED_BANKS))

        offsets = keep.tile([P, S // 16], U16, name="offsets")
        words = [keep.tile([P, T], I32, name="words%d" % o, align_bytes=64) for o in range(PASSES)]
        scales = keep.tile([P, T], U8, name="scales", align_bytes=64)
        slot_words = [keep.tile([P, S], U32, name="slot_words%d" % o, align_bytes=64) for o in range(PASSES)]
        slot_scales = keep.tile([P, S], U8, name="slot_scales", align_bytes=64)
        first_gates = keep.tile([P, PAIR], F32, name="first_gates")
        later_gates = keep.tile([P, S - PAIR], F32, name="later_gates")
        gates = [first_gates] + [later_gates[:, k * PAIR : (k + 1) * PAIR] for k in range(PAIRS - 1)]
        routed = [keep.tile([P, T], F32, name="routed%d" % b) for b in range(BLOCKS)]
        result = [keep.tile([P, T], F32, name="result%d" % b) for b in range(BLOCKS)]

        raw = {}
        grouped = {}
        codes = {}
        planes = {}
        acc = {}

        def load_weights(e, o):
            raw[e, o] = raw_pool.tile([P, HALF], F32, name="raw")
            rows = w[e, o * P * PACK : (o + 1) * P * PACK, :]
            nc.sync.dma_start(out=raw[e, o][:], in_=rows.rearrange("(p j) n -> p (j n)", j=PACK))

        def load_words(o):
            nc.sync.dma_start(out=words[o][:], in_=x_words[o].rearrange("p t r -> p (t r)").bitcast(I32))

        def load_scales(o):
            for r in range(4):
                nc.sync.dma_start(
                    out=scales[:].bitcast(I32)[4 * o + r : P : 32, :],
                    in_=x_scales[o, r:16:4, :].bitcast(I32),
                )

        def cast(engine_copy, dst, e, o, lo, hi):
            src = raw[e, o][:].rearrange("p (t n) -> p t n", t=PACK)[:, :, lo:hi]
            engine_copy(
                out=dst[:, PACK * lo : PACK * hi].rearrange("p (c i t) -> p c t i", i=2, t=PACK),
                in_=src.rearrange("p t (c i) -> p c t i", i=2),
            )

        def multiply(sums, e, at, rhs_words, rhs_scales, cols, o):
            nc.tensor.matmul_mx(
                out=sums,
                lhsT=codes[e][:, at : at + P].bitcast(FP8X4),
                lhsT_scale=planes[e][:, at : at + P],
                rhs=rhs_words[o][:, cols].bitcast(FP8X4),
                rhs_scale=rhs_scales[4 * o : P, cols],
                start=(o == 0),
                stop=(o == PASSES - 1),
            )

        def prepare(e, o):
            if o == 0:
                codes[e] = ring.tile([P, PASSES * N], U32, name="codes", align_bytes=64)
                planes[e] = ring.tile([P, PASSES * N], U8, name="plane", align_bytes=64)
                grouped[e] = ring.tile([P, PASSES * HALF], BF16, name="grouped", align_bytes=64)
            half = grouped[e][:, o * HALF : (o + 1) * HALF]
            split = N - VECTOR_SHARE.get((e, o), 0)
            cast(nc.scalar.copy, half, e, o, 0, split)
            if split < N:
                cast(nc.vector.tensor_copy, half, e, o, split, N)
            lo, hi = QUANTISE_CUTS[o], QUANTISE_CUTS[o + 1]
            nc.vector.quantize_mx(
                out=codes[e][:, lo:hi].bitcast(FP8X4),
                scales=planes[e][:, lo:hi],
                in_=grouped[e][:, PACK * lo : PACK * hi],
            )
            if e < E and o == PASSES - 1:
                k, h = divmod(e, 2)
                slots = slice(e * C, (e + 1) * C)
                for b in range(BLOCKS):
                    if h == 0:
                        acc[k, b] = y_psum.tile([P, PAIR], F32, name="acc%d" % b)
                    for a in range(PASSES):
                        multiply(acc[k, b][:, h * C : (h + 1) * C], e, a * N + b * P, slot_words, slot_scales, slots, a)

        def scatter(k, b, staged, engine_copy):
            engine_copy(out=staged, in_=acc[k, b][:])
            nc.vector.tensor_tensor(
                routed[b][:].indirect(offsets[:, k * PAIR // 16 : (k + 1) * PAIR // 16]), staged, gates[k][:], MULT
            )

        def shared_sums(b, c):
            shared = s_psum.tile([P, BANK], F32, name="shared")
            for o in range(PASSES):
                multiply(shared[:], E, o * N + b * P, words, scales, slice(c * BANK, (c + 1) * BANK), o)
            return shared

        def add_on_vector(b, c, pieces):
            shared = shared_sums(b, c)
            width = BANK // pieces
            for i in range(pieces):
                lo = c * BANK + i * width
                nc.vector.tensor_tensor(
                    result[b][:, lo : lo + width],
                    shared[:, i * width : (i + 1) * width],
                    routed[b][:, lo : lo + width],
                    ADD,
                )
                if pieces > 1:
                    store(b, lo, lo + width)

        def add_on_gpsimd(b, c):
            shared = shared_sums(b, c)
            tokens = slice(c * BANK, (c + 1) * BANK)
            nc.scalar.copy(out=result[b][:, tokens], in_=shared[:])
            nc.gpsimd.tensor_tensor(result[b][:, tokens], result[b][:, tokens], routed[b][:, tokens], ADD)

        def store(b, lo, hi):
            nc.sync.dma_start(out=out[b * P : (b + 1) * P, lo:hi], in_=result[b][:, lo:hi])

        nc.vector.memset(scales[:].bitcast(I32), 0)
        nc.sync.dma_start(offsets[:], offs)
        load_words(0)
        load_scales(0)
        load_words(1)
        load_weights(0, 0)
        load_scales(1)
        load_weights(0, 1)
        load_weights(1, 0)
        load_weights(1, 1)
        nc.sync.dma_start(out=first_gates[:], in_=gate[0:P, 0:PAIR])
        for e in range(2, E + 1):
            for o in range(PASSES):
                load_weights(e, o)
            if e == 3:
                nc.sync.dma_start(out=later_gates[:], in_=gate[0:P, PAIR:S])

        nc.vector.memset(routed[0][:], 0.0)
        for b in range(1, BLOCKS):
            nc.scalar.copy(out=routed[b][:], in_=routed[0][:])

        for o in range(PASSES):
            nc.vector.tensor_copy(slot_words[o][:], words[o][:].bitcast(U32).indirect(offsets[:]))
        nc.vector.tensor_copy(slot_scales[:], scales[:].indirect(offsets[:]))

        for e in range(2):
            for o in range(PASSES):
                prepare(e, o)
        scatter(0, 0, raw[1, 1][:, 0:PAIR], nc.vector.tensor_copy)
        prepare(2, 0)
        scatter(0, 1, raw[2, 0][:, 0:PAIR], nc.scalar.copy)
        prepare(2, 1)
        for k in range(1, PAIRS):
            for o in range(PASSES):
                prepare(2 * k + 1, o)
            scatter(k - 1, 2, raw[2 * k + 1, 1][:, 0:PAIR], nc.scalar.copy)
            for o in range(PASSES):
                prepare(2 * k + 2, o)
                scatter(k, o, raw[2 * k + 2, o][:, 0:PAIR], nc.scalar.copy)

        for c in range(2):
            add_on_vector(0, c, 1)
            add_on_gpsimd(1, c)
        store(0, 0, T // 2)
        for c in range(2, 4):
            add_on_vector(0, c, 1)
        store(0, T // 2, T)
        for c in range(2, 4):
            add_on_vector(1, c, 1)
        store(1, 0, T)
        scatter(PAIRS - 1, 2, routed[0][:, T - BANK : T - BANK + PAIR], nc.scalar.copy)

        for c in range(3):
            add_on_vector(2, c, 1)
            store(2, c * BANK, (c + 1) * BANK)
        add_on_vector(2, 3, 2)
